import numpy as np, ml_dtypes
CORES = [24,25,26,27,28,29,30,31]
N = 8
import mx_ref
BF = ml_dtypes.bfloat16
def gentries(a):
    return np.ascontiguousarray(a.reshape(8, 16, -1).transpose(0, 2, 1)).reshape(8, -1)
def gtable(e):
    e = np.asarray(e); return np.ascontiguousarray(e.reshape(8, -1, 16).transpose(0, 2, 1)).reshape(128, -1).astype(np.int32)
def gcols(t, e):
    v = np.concatenate([t.reshape(8, 16, -1, 4), np.zeros((8, 16, 1, 4), BF)], axis=2)
    return np.ascontiguousarray(np.stack([v[g][:, e[g]] for g in range(8)])).reshape(128, -1)
def tile(rs):
    return np.stack(rs, axis=2).reshape(128, -1).astype(BF)
def pick(q, e):
    c = np.concatenate([q[0].reshape(128, -1, 4), np.zeros((128, 1, 4), np.uint8)], axis=1); s = np.concatenate([q[1], np.ones((16, 1), np.uint8)], axis=1)
    return (np.ascontiguousarray(c[:, e].reshape(128, -1)), np.ascontiguousarray(s[:, e]))
def join(*qs):
    return (np.concatenate([q[0] for q in qs], axis=1), np.concatenate([q[1] for q in qs], axis=1))
def put(q, e, v):
    c, s = q[0].reshape(128, -1, 4).copy(), q[1].copy(); c[:, e] = v[0].reshape(128, -1, 4); s[:, e] = v[1]
    return (c.reshape(128, -1), s)
def pk(c, s):
    return (np.ascontiguousarray(c), mx_ref.live(s))
def emit(q):
    return q[0], q[1]
def packed(v, rng):
    q = [mx_ref.quantize(np.ascontiguousarray(v[r])) for r in range(N)]
    return np.stack([a for a, b in q]), np.stack([mx_ref.plane(b, rng) for a, b in q])
def values_of_codes():
    e, c = np.zeros((128, 128, 4), np.float32), np.zeros((128, 2, 4), np.uint8)
    e[np.arange(128), np.arange(128), 0] = 1
    c[:127, :, 0] = np.arange(256).reshape(2, 128).T[:127]
    return mx_ref.matmul(mx_ref.quantize(e.reshape(128, 512).astype(BF)), (c.reshape(128, 8), np.full((16, 2), 127, np.uint8))).T.reshape(-1).astype(np.float64)
CODE_VALUE, SCALE_VALUE = values_of_codes(), 2.0 ** (np.arange(256) - 127.0)
def decode(q):
    return (CODE_VALUE[q[0]].reshape(16, 8, -1, 4) * SCALE_VALUE[q[1]][:, None, :, None] + 0.0).reshape(128, -1).astype(np.float32)
def f(rng, *shape):
    return mx_ref.flush((rng.standard_normal(shape, dtype=np.float32) * np.exp2(rng.integers(-2, 3, shape[:-1] + (1,)))).astype(BF))
def wide(rng, *shape, cols=0):
    v = rng.standard_normal(shape, dtype=np.float32) * np.exp2(rng.integers(-12, 13, shape)).astype(np.float32)
    if cols: v *= np.repeat(np.exp2(rng.integers(-cols, cols + 1, shape[:-2] + (1, shape[-1] // 4))) * (rng.random(shape[:-2] + (1, shape[-1] // 4)) > 0.0625), 4, axis=-1).astype(np.float32)
    return mx_ref.flush(v.astype(BF))
C, H, R = 256, 96, 3
def numbers_of(rng):
    return {"x": np.array(f(rng, N, 128, 4 * C)), "u": np.array(f(rng, N, 128, 512)), "v": np.array(f(rng, N, 128, 512))}
def orders(rng):
    return np.argsort(rng.random((N, 8, C)), axis=2)
def bonds(e):
    return np.stack([gtable(e[r]) for r in range(N)])
def layers(rng, still=()):
    w = np.array(f(rng, N, 128, 2048)).reshape(N, 8, 16, 4, 8, 16, 4)
    for i in still:
        w[:, :, i] = 0
        w[:, :, :, :, :, i] = 0
    return w
def weights(rng, w):
    c, p = packed(np.ascontiguousarray(w).reshape(N, 128, 2048), rng)
    return {"wc": c, "ws": p}
def chosen(rng, n):
    k, a = np.arange(8 * n), np.zeros((8, C), bool)
    a[k % 8, k // 4] = True
    return a[:, rng.permutation(C)]
def crowd(rng):
    n, o = H + 1, rng.permutation(C)
    full, half, none, rest = o[:48], o[48:48 + n], o[48 + n:48 + 2 * n], o[48 + 2 * n:]
    a, e = np.zeros((8, C), bool), np.zeros((8, C), np.int64)
    a[:, full] = True
    for j in range(n): a[(j + 1 + rng.permutation(7)[:4]) % 8, half[j]] = True
    for g in range(8):
        b = np.concatenate([half[g::8], rng.permutation(np.delete(half, np.arange(g, n, 8)))])
        e[g, none] = rng.permutation(half)
        e[g, b[:48]] = rng.permutation(full)
        e[g, np.concatenate([b[48:], full])] = rng.permutation(none)
        e[g, rest] = rng.permutation(rest)
    return a, e
def faint():
    k = 2.0 ** -np.arange(4.0, 28.0)
    t = np.zeros((128, 24, 4), np.float32)
    t[0, :, 0] = 1.96875
    t[7, :, 0] = k
    once = decode(mx_ref.quantize(t.reshape(128, 96).astype(BF)))
    again = decode(mx_ref.quantize(once.astype(BF)))
    i = int(np.argmax((once[7, ::4] > 0) & (again[7, ::4] == 0)))
    assert once[7, 4 * i] == k[i] and again[7, 4 * i] == 0
    return k[i]
def plant(d, s):
    x = d["x"].reshape(N, 8, 16, C, 4)
    x[:, :, 0] = 0
    x[:, :, 0, :, 0] = s.astype(np.float32).astype(BF)
    u = d["u"].reshape(N, 128, 128, 4)
    u[:, :, ::16] = 0
    for h in range(0, 128, 16): u[:, h, h, 0] = 1
def setup_inputs(rng):
    return {**numbers_of(rng), "m": bonds(orders(rng)), **weights(rng, layers(rng))}
def setup_inputs_slots(rng):
    d = numbers_of(rng)
    e, s, c, h = orders(rng), np.zeros((N, 8, C)), int(rng.integers(4)), H // 2
    for r in range(N):
        k = (r + c) % 4
        if k == 0:
            a = chosen(rng, H)
            for g in rng.permutation(8)[:4]: a[g, rng.choice(np.flatnonzero(a[g]))] = False
        elif k == 1: a = chosen(rng, H + 1)
        elif k == 2:
            o = rng.permutation(C)
            a = np.zeros((8, C), bool)
            a[:, o[:h]] = True
            for g in range(8):
                e[r, g, o[h:2 * h]] = rng.permutation(o[:h])
                e[r, g, o[2 * h:3 * h]] = rng.permutation(o[h:2 * h])
                e[r, g, o[:h]] = rng.permutation(o[2 * h:3 * h])
                e[r, g, o[3 * h:]] = rng.permutation(o[3 * h:])
        else: a, e[r] = crowd(rng)
        s[r] = np.where(a, 1.0, -1.0 * rng.integers(0, 2, (8, C)))
    plant(d, s)
    x = d["x"].reshape(N, 8, 16, C, 4)
    x[:, :, 8:11] = 0
    x[:, :, 8, :, 0] = 1
    u = d["u"].reshape(N, 128, 128, 4)
    for i in range(0, 128, 16): u[:, i + 10, i, 0] = 1
    w, o = layers(rng, (0, 8, 9, 10)), rng.permutation(8)
    w[:, :, 8, 0, :, 9, 0] = 4
    for r in range(N):
        for j in range(8): w[r, :, 9, 0, o[(2 * r + j) % 8], 10, 0] = 512 if j < 4 else -512
    return {**d, "m": bonds(e), **weights(rng, w)}
def setup_inputs_near(rng):
    d = numbers_of(rng)
    x = d["x"].astype(np.float32).reshape(N, 8, 16, C, 4)
    x[:, :, :2] = 0
    x[:, :, 8:] = 0
    c = rng.choice([-1.0, 1.0], (N, 8, C))
    a = rng.choice([-1.0, 0.0, 1.0, 1.0], (3, N, 8, C))
    x[:, :, 0, :, 0] = c
    x[:, :, 1, :, 0] = -c
    x[:, :, 8, :, 0] = a[0] * 2.0 ** -30
    x[:, :, 9, :, 0] = a[1] * 2.0 ** -23
    x[:, :, 10, :, 0] = a[2] * 1.125 * 2.0 ** -30
    x[:, :, 11, :, 0] = a[2] * -1.0 * 2.0 ** -30
    u = d["u"].reshape(N, 128, 128, 4)
    u[:, :, ::16] = 0
    o = rng.permutation(N) % 3
    for r in range(N):
        if o[r] == 0:
            for g in rng.permutation(8)[:4]: x[r, g, 8, rng.integers(C), 0] = 2.0 ** 30 * rng.choice([-1.0, 1.0])
        for h in range(0, 128, 16):
            if o[r] == 0: u[r, h + 8, h, 0] = 2.0 ** -30
            elif o[r] == 1:
                u[r, h + 10, h, 0] = 1.125 * 2.0 ** -30
                u[r, h + 11, h, 0] = 1.25 * 2.0 ** -30
            else:
                for i in (0, 1, 9): u[r, h + i, h, 0] = 1
    return {"x": x.reshape(N, 128, 4 * C).astype(BF), "u": d["u"], "v": d["v"], "m": bonds(orders(rng)), **weights(rng, layers(rng, (0, 1, 8, 9, 10, 11, 12, 13, 14, 15)))}
def setup_inputs_late(rng):
    d = numbers_of(rng)
    k = np.argsort(rng.random((N, 8, C)), axis=1)
    known = k < 4 + (rng.permutation(N) % 2)[:, None, None]
    plant(d, np.where(k == 0, 0.0, np.where(known, 1.0, -1.0)))
    x = d["x"].reshape(N, 8, 16, C, 4)
    n = (N, 8, 8, C, 4)
    a = (1 + (2 * rng.integers(0, 64, n) + 1) * 2.0 ** -7) * np.exp2(rng.integers(-14, -7, n))
    a[:, :, 0, :, 0] = 1.96875
    x[:, :, 8:] = (a * (2.0 * rng.integers(0, 2, n) - 1.0)).astype(np.float32).astype(BF)
    x[:, :, 15, :, 0] = np.where(k == 0, faint(), 0.0).astype(np.float32).astype(BF)
    u = d["u"].reshape(N, 128, 128, 4)
    for h in range(0, 128, 16): u[:, h + 15, h, 0] = 1
    return {**d, "m": bonds(orders(rng)), **weights(rng, layers(rng))}
def setup_inputs_ends(rng):
    d = numbers_of(rng)
    x, e, c, i = np.zeros((N, 8, 16, C, 4)), orders(rng), int(rng.integers(4)), np.arange(128)
    u, v = d["u"].reshape(N, 128, 128, 4), d["v"]
    u[:, :, ::16] = 0
    w = np.zeros((N, 128, 4, 128, 4), np.float32)
    for r in range(N):
        k = (r + c) % 4
        a = (0.75 + 0.25 * rng.random((8, 16, C, 4))) * 2.0 ** 30
        for j in range(4): w[r, i, j, i, j] = 2.0 ** -30
        if k == 0:
            x[r] = a * rng.choice([-1.0, 1.0], C)[:, None]
            s = np.where(rng.permutation(8) < 5, 1.0, -1.0)
            for g in range(8): u[r, :, 16 * g] = s[g] * 2.0 ** 30
            e[r] = np.arange(C)[::-1]
            v[r] = (2.0 ** 30 * rng.choice([-1.0, 1.0], (128, 512))).astype(np.float32).astype(BF)
            n = i[i % 16 < 8]
            for j in range(4): w[r, n, j, n, j] = -1
        elif k == 1:
            x[r] = (1 + 0.25 * rng.integers(0, 4, (8, 16, C, 4))) * 2.0 ** -30
            x[r, :, :8] *= 2.0
            u[r, :, ::16] = 2.0 ** -30
            e[r] = np.arange(C)
            v[r] = (2.0 ** -30 * rng.choice([-1.0, 1.0], (128, 512))).astype(np.float32).astype(BF)
        elif k == 2:
            x[r] = -a
            u[r, :, ::16] = 2.0 ** 30
        else:
            x[r] = a * np.where(chosen(rng, H), 1.0, -1.0)[:, None, :, None]
            for g in range(8): u[r, 16 * g:16 * g + 16, 16 * g] = 2.0 ** 30
            e[r] = rng.permutation(C)
    return {"x": x.astype(np.float32).reshape(N, 128, 4 * C).astype(BF), "u": d["u"], "v": v, "m": bonds(e), **weights(rng, w.astype(BF))}
def setup_inputs_spread(rng):
    d = setup_inputs(rng)
    d["x"] = wide(rng, N, 128, 4 * C, cols=6)
    return d
def check_inputs(d):
    b = []
    for k in ("x", "u", "v"):
        a = np.abs(d[k].astype(np.float32))
        if not (np.isfinite(a).all() and ((a == 0) | (a >= 2.0 ** -30) & (a <= 2.0 ** 30)).all()): b.append("a value of " + k)
    none, least, most = [emit(mx_ref.quantize(np.full((128, 16), k, np.float32).astype(BF)))[1][0, 0] for k in (0.0, 2.0 ** -30, 2.0 ** 30)]
    for r in range(N):
        if (np.sort(gentries(d["m"][r]), axis=1) != np.arange(C)).any(): b.append("m: a list that is no permutation")
        if ((d["wc"][r] == 0x7F) | (d["wc"][r] == 0xFF)).any(): b.append("wc: a code that is no number")
        s = mx_ref.live(d["ws"][r])
        if ((s != none) & ((s < least) | (s > most))).any(): b.append("ws: a scale out of range")
    return b
def waves(s, to):
    w = np.where(s > 0, 1, 4)
    for t in (2, 3):
        licensed = np.count_nonzero(w < 4, axis=0) >= 5
        w = np.where((w == 4) & licensed[to], t, w)
    return w
def reference(x, u, v, m, wc, ws):
    qu = [mx_ref.quantize(u[r]) for r in range(N)]
    lay = [pk(wc[r], ws[r]) for r in range(N)]
    now = [x[r] for r in range(N)]
    lists = np.stack([gentries(m[r]) for r in range(N)])
    for t in range(R):
        to = np.roll(lists, -t, axis=1)
        own, wave, sent = [], [], []
        for r in range(N):
            q = mx_ref.quantize(now[r])
            own.append(decode(q).astype(BF))
            wave.append(waves(mx_ref.matmul(qu[r], q)[::16], to[r]))
            o = np.argsort(np.where(wave[r] < 4, 3 - wave[r], 3), axis=1, kind="stable")[:, :H]
            e = np.where(np.take_along_axis(wave[r], o, axis=1) < 4, o, -1)
            sent.append(mx_ref.quantize(gcols(own[r], e)))
        for r in range(N):
            guests = decode(sent[(r - 1) % N]).astype(BF)
            k = np.argsort(np.argsort(wave[r] < 4, axis=1, kind="stable"), axis=1)
            e = np.where(wave[r] == 1, np.arange(C), np.where(wave[r] < 4, to[r], C + k % H))
            z = gcols(np.concatenate([own[r], guests], axis=1), e)
            q = mx_ref.quantize(z)
            made = tile([mx_ref.matmul(pick(lay[r], np.arange(128 * b, 128 * b + 128)), q) * np.float32(0.03125) + z[:, b::4].astype(np.float32) for b in range(4)])
            now[r] = gcols(made, np.argsort(to[r], axis=1))
    y, wv = np.zeros((N, 128, C), np.float32), np.zeros((N, 8, C), np.float32)
    oc, osc = np.zeros((N, 128, 4 * C), np.uint8), np.zeros((N, 16, C), np.uint8)
    for r in range(N):
        q = mx_ref.quantize(now[r])
        y[r] = mx_ref.matmul(mx_ref.quantize(v[r]), q)
        wv[r] = wave[r]
        oc[r], osc[r] = emit(q)
    return {"y": y, "wv": wv, "oc": oc, "osc": osc}

@@ -1,0 +1,334 @@
+from concourse.mybir import dt, AluOpType, ActivationFunctionType
+
+R = 3
+BIG = 512.0
+
+
+def _scratch():
+    s = {}
+
+    def sb(d, w, names):
+        for n in names.split():
+            s[n] = ("sbuf", [128, w], d)
+
+    for w, names in ((128, "u u16 v ta tb ft"), (256, "x c p z f0 f1 f2 h0 h1 h2"), (512, "w e")):
+        for n in names.split():
+            s["q" + n] = ("sbuf", [128, w], "float8_e4m3fn_x4")
+            s["s" + n] = ("sbuf", [128, w], "uint8")
+    sb("bfloat16", 2048, "et")
+    sb("bfloat16", 1408, "fg")
+    sb("bfloat16", 1024, "x0 z xt ct pt")
+    sb("bfloat16", 512, "u0 v0 ta tb ft sl")
+    sb("bfloat16", 272, "hp0 hp1 hp2 hp3")
+    sb("bfloat16", 256, "row msk rsI rs lic1 lic2 d wa wb iv z320 z321 z322 z323 tt0 tt1 tt2 tt3")
+    sb("bfloat16", 128, "ones neg ident nb nb2 rr rr2")
+    sb("uint16", 16, "mo0 mo1 mo2 inv0 inv1 inv2 pos off0 off1 off2 off3")
+    sb("uint16", 6, "slot0 slot1 slot2 land0 land1 land2")
+    sb("uint16", 8, "pick8")
+    sb("int32", 8, "pick8i")
+    sb("int32", 16, "mi0 mi1 mi2 ipI")
+    sb("int32", 256, "mskI")
+    sb("float32", 16, "ic leg m16")
+    sb("float32", 32, "m32")
+    sb("float32", 48, "mf")
+    sb("float32", 64, "zz cum pp")
+    sb("float32", 192, "ll")
+    sb("float32", 256, "wrow yb")
+    for n in "k0 k1 k2 k3 b0 b1 b2 b3".split():
+        s[n] = ("psum", [128, 512], "float32")
+    return s
+
+
+SCRATCH = _scratch()
+LOADS = ["u", "xa", "xb", "v", "wc", "ws", "m0", "m1", "m2"]
+SEMAPHORES = ["sV", "sT", "sA", "sG", "loc", "st", "st2"] + ["ld_" + n for n in LOADS] + ["ah0", "ah1", "ah2", "al0", "al1", "al2"]
+
+
+def rank_program(g, core, T, topo):
+    rank = T.rank_of(core)
+    if rank is None:
+        return
+    A = AluOpType
+    COPY = ActivationFunctionType.Copy
+    nxt = T.cores[(rank + 1) % len(T.cores)]
+    rid, pid = topo.addr(nxt)[0], topo.addr(nxt)[1]
+    mask, neng = topo.mask(core, nxt), len(topo.engines(core, nxt))
+    queues = {"V": g.vector, "T": g.tensor, "A": g.scalar, "G": g, "S": g.sync}
+    known = {q: {} for q in queues}
+    count, writer, readers = {}, {}, {}
+
+    def order(q, need):
+        best = {}
+        for e in need:
+            if known[q].get(e[0], 0) < e[1] and (e[0] not in best or best[e[0]][1] < e[1]):
+                best[e[0]] = e
+        for s in list(best):
+            if any(o != s and best[o][2].get(s, 0) >= best[s][1] for o in best):
+                del best[s]
+        for s in best:
+            _, v, c = best[s]
+            queues[q].wait_ge(T.sem[s], v)
+            for k in c:
+                known[q][k] = max(known[q].get(k, 0), c[k])
+            known[q][s] = max(known[q].get(s, 0), v)
+
+    def op(q, fn, r=(), w=(), sem=None, inc=1):
+        need = []
+        for k in r:
+            if k in writer:
+                need.append(writer[k])
+        for k in w:
+            if k in writer:
+                need.append(writer[k])
+            need += [e for qq, e in readers.get(k, {}).items() if qq != q]
+        order(q, need)
+        i = fn()
+        s = sem or "s" + q
+        i.then_inc(T.sem[s], inc)
+        count[s] = count.get(s, 0) + inc
+        c = dict(known[q])
+        c[s] = count[s]
+        e = (s, count[s], c)
+        for k in r:
+            readers.setdefault(k, {})[q] = e
+        for k in w:
+            writer[k] = e
+            readers[k] = {}
+
+    def V(fn, r="", w=""):
+        op("V", fn, r.split(), w.split())
+
+    def act(out, in_, r, w, **kw):
+        op("A", lambda: g.scalar.activation(out, in_, COPY, **kw), r.split(), w.split())
+
+    def ts(out, in0, s1, s2, op0, op1=None):
+        if op1 is None:
+            return lambda: g.vector.tensor_scalar(out, in0, s1, None, op0)
+        return lambda: g.vector.tensor_scalar(out, in0, s1, s2, op0, op1)
+
+    def tt(out, a, b, o):
+        return lambda: g.vector.tensor_tensor(out, a, b, o)
+
+    def cp(out, a):
+        return lambda: g.vector.tensor_copy(out, a)
+
+    def fill(ap, v):
+        return lambda: g.vector.memset(ap, v)
+
+    def scan(out, a, b, init, o0, o1):
+        return lambda: g.vector.tensor_tensor_scan(out, a, b, init, o0, o1)
+
+    def quant(n, src, a, b, r, tok):
+        V(lambda: g.vector.quantize_mx(T["q" + n][:, a:b], T["s" + n][:, a:b], src), r, tok)
+
+    def mm(bank, ln, la, rn, ra, rb, r):
+        op("T", lambda: g.tensor.matmul_mx(T[bank][:, 0:rb - ra], T["q" + ln][:, la:la + 128], T["s" + ln][:, la:la + 128],
+                                           T["q" + rn][:, ra:rb], T["s" + rn][:, ra:rb], True, True), r.split(), [bank])
+
+    def dma(q, out, in_, sem, r="", w=""):
+        op(q, lambda: queues[q].dma_start(out, in_), r.split(), w.split(), sem, 16)
+
+    def wrapped(src, n, tok):
+        V(scan(T.wa[:, 0:n], src, T.msk[:, 0:n], BIG, A.min, A.max), tok + " msk", "wa")
+        V(scan(T.wb[:, 0:n], T.rs[:, 0:n], T.wa[:, 0:n], BIG, A.max, A.min), "wa rs", "wb")
+
+    def const(name, pat, base, ch, in_=None, cmp=None, fv=None):
+        if in_ is None:
+            small = SCRATCH[name][2] != "int32"
+            op("G", lambda: g.iota(T[name][:], pat, base, ch, allow_small_or_imprecise_dtypes=small), [], [name])
+        else:
+            op("G", lambda: g.affine_select(T[name][:], T[in_][:], pat, cmp, fv, base, ch), [in_], [name])
+
+    dma("S", T.u0[:], T.u[:], "ld_u", "", "u0")
+    dma("A", T.x0[:, 0:512], T.x[:, 0:512], "ld_xa", "", "x0a")
+    dma("S", T.mi0[:], T.m[:], "ld_m0", "", "mi0")
+    dma("A", T.x0[:, 512:1024], T.x[:, 512:1024], "ld_xb", "", "x0b")
+    dma("S", T.qw[:].bitcast(dt.uint8), T.wc[:], "ld_wc", "", "qw")
+    dma("S", T.sw[:], T.ws[:], "ld_ws", "", "sw")
+    for t in (1, 2):
+        n = 16 * t
+        dma("S", T["mi%d" % t][0:128 - n, :], T.m[n:128, :], "ld_m%d" % t, "", "mi%da" % t)
+        dma("S", T["mi%d" % t][128 - n:128, :], T.m[0:n, :], "ld_m%d" % t, "", "mi%d" % t)
+    dma("S", T.v0[:], T.v[:], "ld_v", "", "v0")
+
+    V(fill(T.ones[:], 1.0), "", "ones")
+    V(fill(T.neg[:], -1.0), "", "neg")
+    const("pick8i", [[16, 8]], 0, 0)
+    const("ident", [[-1, 128]], 0, 1, "ones", A.is_equal, 0.0)
+    const("mskI", [[1, 256]], 128, -1)
+    const("rsI", [[0, 16], [1, 16]], 0, 0)
+    const("nb", [[-16, 8], [0, 16]], 0, 1, "neg", A.is_ge, 0.0)
+    const("nb2", [[16, 8], [0, 16]], 15, -1, "nb", A.is_ge, 0.0)
+    const("rr", [[-1, 128]], 0, 1, "nb2", A.is_gt, 0.0)
+    const("rr2", [[-1, 128]], 0, 1, "rr", A.not_equal, -1024.0)
+    const("row", [[1, 256]], 0, 0)
+    const("ipI", [[0, 16]], 0, 1)
+    const("ic", [[16, 16]], 0, 0)
+    V(fill(T.ct[:], 0.0), "", "ct")
+    V(fill(T.ct[:, 0:512:4], 0.0625), "", "ct")
+    V(fill(T.ct[:, 514:1024:4], 0.0625), "", "ct")
+    quant("c", T.ct[:], 0, 256, "ct", "qc")
+    V(fill(T.ta[:], 0.0), "", "ta")
+    V(cp(T.pick8[:], T.pick8i[:]), "pick8i", "pick8")
+    V(fill(T.et[:], 0.0), "", "et")
+    quant("u", T.u0[:], 0, 128, "u0", "qu")
+    V(cp(T.qu16[:, 0:128].bitcast(dt.uint32), T.qu[:, 0:128].bitcast(dt.uint32).indirect(T.pick8[:, 0:8])), "qu pick8", "qu16")
+    V(cp(T.su16[:, 0:128], T.su[:, 0:128].indirect(T.pick8[:, 0:8])), "qu pick8", "su16")
+
+    def late_constants():
+        for b in range(4):
+            V(cp(T.et[:, 512 * b + b:512 * b + 512:4], T.ident[:]), "ident et", "et%d" % b)
+        quant("e", T.et[:], 0, 512, "et et0 et1 et2 et3", "qe")
+        V(fill(T.tb[:], 0.0), "", "tb")
+        V(cp(T.mo0[:], T.mi0[:]), "mi0", "mo0")
+
+    def later_constants():
+        V(ts(T.mskI[:], T.mskI[:], 15, None, A.bitwise_and), "mskI", "mskI")
+        V(ts(T.msk[:], T.mskI[:], 0.0, BIG, A.is_gt, A.mult), "mskI", "msk")
+        V(ts(T.rs[:], T.rsI[:], 0.0, BIG, A.is_equal, A.mult), "rsI", "rs")
+        V(fill(T.ft[:], 0.0), "", "ft")
+        V(fill(T.pt[:], 0.0), "", "pt")
+        V(cp(T.pt[:, 0:512:4], T.rr2[:]), "rr2", "pt")
+        V(ts(T.pt[:, 512:1024:4], T.nb2[:], -1.0, None, A.mult), "nb2", "pt")
+        quant("p", T.pt[:], 0, 256, "pt", "qp")
+        V(fill(T.zz[:], 0.0), "", "zz")
+        V(ts(T.ipI[:], T.ipI[:], 15, None, A.bitwise_and), "ipI", "ipI")
+        V(tt(T.leg[:], T.ipI[:], T.ic[:], A.add), "ipI ic", "leg")
+        V(ts(T.pp[:, 48:64], T.leg[:], -767.0, None, A.add), "leg", "pc")
+        V(cp(T.mf[:, 0:16], T.mi0[:]), "mi0", "mf0")
+
+    def last_constants():
+        for b in range(4):
+            V(fill(T["hp%d" % b][:, 256:272], 0.0), "", "hz%d" % b)
+        for t in (1, 2):
+            V(cp(T["mo%d" % t][:], T["mi%d" % t][:]), "mi%d" % t, "mo%d" % t)
+            V(cp(T.mf[:, 16 * t:16 * t + 16], T["mi%d" % t][:]), "mi%d" % t, "mf%d" % t)
+        quant("v", T.v0[:], 0, 128, "v0", "qv")
+
+    even = slice(0, 512, 2)
+    xs = "xs0 xs1 xs2 xs3"
+    for t in range(R):
+        mo = T["mo%d" % t][:, 0:16]
+        mot = " mo%d" % t
+        X = T.xt if t else T.x0
+        quant("x", X[:, 0:512], 0, 128, xs if t else "x0a", "qxa")
+        quant("x", X[:, 512:1024], 128, 256, xs if t else "x0b", "qxb")
+        mm("k0", "u16", 0, "x", 0, 128, "qu16 su16 qxa")
+        mm("k1", "u16", 0, "x", 128, 256, "qu16 su16 qxb")
+
+        def unpack(b):
+            mm("b%d" % b, "e", 128 * b, "x", 0, 256, "qe qxa qxb")
+            act(T.fg[:, b:1024:4], T["b%d" % b][:, 0:256], "b%d" % b, "f%d" % b)
+        if t:
+            unpack(0)
+        for h in (0, 1):
+            V(ts(T.ta[:, 256 * h:256 * h + 256:2], T["k%d" % h][:, 0:128], 0.0, 1.25, A.is_gt, A.mult), "ta k%d" % h, "ta%d" % h)
+        quant("ta", T.ta[:], 0, 128, "ta ta0 ta1", "qta")
+        mm("k2", "c", 0, "ta", 0, 128, "qc qta")
+        mm("k3", "c", 128, "ta", 0, 128, "qc qta")
+        if t == 0:
+            late_constants()
+            unpack(0)
+        for b in (1, 2, 3):
+            unpack(b)
+        V(ts(T.lic1[:, 0:256:2], T.k2[:, 0:128], 5.5, 1.125, A.is_ge, A.mult), "k2", "lic1a")
+        V(ts(T.lic1[:, 1:256:2], T.k3[:, 0:128], 5.5, 1.125, A.is_ge, A.mult), "k3", "lic1b")
+        V(tt(T.tb[:, even], T.lic1[:, 0:256].indirect(mo), T.ta[:, even], A.max), "lic1a lic1b ta0 ta1 tb" + mot, "tbv")
+        quant("tb", T.tb[:], 0, 128, "tb tbv", "qtb")
+        mm("k2", "c", 0, "tb", 0, 128, "qc qtb")
+        mm("k3", "c", 128, "tb", 0, 128, "qc qtb")
+        if t == 0:
+            later_constants()
+        V(ts(T.lic2[:, 0:256:2], T.k2[:, 0:128], 5.5, 0.875, A.is_ge, A.max), "k2", "lic2a")
+        V(ts(T.lic2[:, 1:256:2], T.k3[:, 0:128], 5.5, 0.875, A.is_ge, A.max), "k3", "lic2b")
+        V(tt(T.d[:], T.lic2[:, 0:256].indirect(mo), T.tb[:, even], A.max), "lic2a lic2b tbv" + mot, "d")
+        wrapped(T.d[:], 256, "d")
+        for k, code in enumerate((1.0, 1.125, 1.25, 0.875)):
+            V(ts(T.ft[:, 64 * k:64 * k + 64:4], T.wb[:, 15:256:16], code, None, A.is_equal), "wb ft", "ft%d" % k)
+        quant("ft", T.ft[:], 0, 128, "ft ft0 ft1 ft2 ft3", "qft")
+        mm("k1", "p", 128, "ft", 0, 128, "qp qft")
+        mm("k0", "p", 0, "ft", 0, 128, "qp qft")
+        quant("f%d" % t, T.fg[:, 0:1024], 0, 256, "f0 f1 f2 f3", "qf")
+        order("G", [writer["qf"]])
+        g.remote_dma(T["qh%d" % t][:].bitcast(dt.uint8), T["qf%d" % t][:].bitcast(dt.uint8), T.sem["ah%d" % t], T.sem.loc, pid, rid, mask)
+        g.remote_dma(T["sh%d" % t][:], T["sf%d" % t][:], T.sem["ah%d" % t], T.sem.loc, pid, rid, mask)
+        V(fill(T.sl[:, 0:96], 256.0), "", "sl")
+        V(scan(T.cum[:], T.k1[:, 0:64], T.zz[:], 0.0, A.add, A.add), "k1 zz", "cum")
+        V(tt(T.pp[:, 0:48], T.cum[:, 0:48], T.k0[:, 0:48], A.add), "cum k0", "pp")
+        V(tt(T.m32[:], T.pp[:, 0:32], T.pp[:, 32:64], A.min), "pp pc", "m32")
+        V(tt(T.m16[:], T.m32[:, 0:16], T.m32[:, 16:32], A.min), "m32", "m16")
+        V(ts(T.pos[:], T.m16[:], 1023.0, None, A.add), "m16", "pos")
+        V(cp(T.sl[:, 0:512].indirect(T.pos[:, 0:16]), T.row[:, 0:256]), "pos row", "sl")
+        wrapped(T.sl[:, 0:96], 96, "sl")
+        V(cp(T["slot%d" % t][:, 0:6], T.wb[:, 15:96:16]), "wb", "slot")
+        order("G", [writer["slot"]])
+        g.remote_dma(T["land%d" % t][:], T["slot%d" % t][:], T.sem["al%d" % t], T.sem.loc, pid, rid, mask)
+        L = [T.ll[:, 16 * k:16 * k + 16] for k in range(12)]
+        F3, F2, F1, F4 = [T.ft[:, 64 * k:64 * k + 64:4] for k in range(4)]
+        V(tt(L[0], F1, T.leg[:], A.mult), "ft2 leg", "l0")
+        V(tt(L[1], F2, F3, A.add), "ft0 ft1", "l1")
+        V(tt(L[3], T.cum[:, 48:64], T.k0[:, 48:64], A.add), "cum k0", "l3")
+        V(tt(L[2], L[1], T.mf[:, 16 * t:16 * t + 16], A.mult), "l1 mf%d" % t, "l2")
+        V(ts(L[4], L[3], T.cum[:, 47:48], 1279.0, A.subtract, A.add), "l3 cum", "l4")
+        V(tt(L[5], L[0], L[2], A.add), "l0 l2", "l5")
+        V(ts(L[6], L[4], 352.0, -96.0, A.is_ge, A.mult), "l4", "l6")
+        V(ts(L[7], L[4], 448.0, -96.0, A.is_ge, A.mult), "l4", "l7")
+        V(tt(L[8], L[4], L[6], A.add), "l4 l6", "l8")
+        V(tt(L[9], L[8], L[7], A.add), "l8 l7", "l9")
+        V(tt(L[10], L[9], F4, A.mult), "l9 ft3", "l10")
+        V(tt(L[11], L[5], L[10], A.add), "l5 l10", "l11")
+        for b in range(4):
+            V(ts(T["off%d" % b][:], L[11], 4.0, float(b), A.mult, A.add), "l11", "off%d" % b)
+        if t == 0:
+            last_constants()
+        V(cp(T.iv[:, 0:256].indirect(mo), T.row[:, 0:256]), "row" + mot, "iv")
+        wrapped(T.iv[:], 256, "iv")
+        V(cp(T["inv%d" % t][:, 0:16], T.wb[:, 15:256:16]), "wb", "inv")
+        if t == R - 1:
+            act(T.wrow[:], T.d[:], "d", "wrow", bias=11.0, scale=-8.0)
+            dma("S", T.wv[:], T.wrow[0:128:16, :], "st", "wrow")
+        writer["hh"] = ("ah%d" % t, 2 * neng, {})
+        writer["land"] = ("al%d" % t, neng, {})
+        for b in range(4):
+            mm("b%d" % b, "e", 128 * b, "h%d" % t, 0, 256, "qe hh")
+            act(T["hp%d" % b][:, 0:256], T["b%d" % b][:, 0:256], "b%d" % b, "hp%d" % b)
+        for b in (0, 2, 1, 3):
+            src, out = T["hp%d" % b][:, 0:272].indirect(T["land%d" % t][:, 0:6]), T.fg[:, 1024 + b:1408:4]
+            r, w = "hp%d hz%d land" % (b, b), "g%d" % b
+            if b < 2:
+                V(cp(out, src), r, w)
+            else:
+                act(out, src, r, w)
+        for b in (0, 2, 1, 3):
+            src, out = T.fg[:, 0:1408].indirect(T["off%d" % b][:, 0:16]), T.z[:, b:1024:4]
+            r, w = "f0 f1 f2 f3 g0 g1 g2 g3 off%d" % b, "z%d" % b
+            if b < 2:
+                V(cp(out, src), r, w)
+            else:
+                act(out, src, r, w)
+        quant("z", T.z[:], 0, 256, "z0 z1 z2 z3", "qz")
+        for b in range(4):
+            mm("b%d" % b, "w", 128 * b, "z", 0, 256, "qw sw qz")
+        for b in (0, 1):
+            V(ts(T["z32%d" % b][:], T.z[:, b:1024:4], 32.0, None, A.mult), "z%d" % b, "z32%d" % b)
+        for b in (2, 3):
+            act(T["z32%d" % b][:], T.z[:, b:1024:4], "z%d" % b, "z32%d" % b, scale=32.0)
+        for b in range(4):
+            V(tt(T["tt%d" % b][:], T["b%d" % b][:, 0:256], T["z32%d" % b][:], A.add), "b%d z32%d" % (b, b), "tt%d" % b)
+            src, out = T["tt%d" % b][:, 0:256].indirect(T["inv%d" % t][:, 0:16]), T.xt[:, b:1024:4]
+            if b == 3:
+                V(ts(out, src, 0.03125, None, A.mult), "inv tt%d" % b, "xs%d" % b)
+            else:
+                act(out, src, "inv tt%d" % b, "xs%d" % b, scale=0.03125)
+    for h, k in ((0, "qxa"), (1, "qxb")):
+        quant("x", T.xt[:, 512 * h:512 * h + 512], 128 * h, 128 * h + 128, xs, k)
+        dma("S", T.oc[:, 512 * h:512 * h + 512], T.qx[:, 128 * h:128 * h + 128].bitcast(dt.uint8), "st", k)
+        mm("k%d" % h, "v", 0, "x", 128 * h, 128 * h + 128, "qv " + k)
+    for k in range(4):
+        dma("A", T.osc[4 * k:4 * k + 4, :], T.sx[32 * k:32 * k + 4, :], "st2", "qxa qxb")
+    for h in (0, 1):
+        V(cp(T.yb[:, 128 * h:128 * h + 128], T["k%d" % h][:, 0:128]), "k%d" % h, "yb%d" % h)
+        dma("S", T.y[:, 128 * h:128 * h + 128], T.yb[:, 128 * h:128 * h + 128], "st", "yb%d" % h)
+    g.wait_ge(T.sem.loc, 3 * R * neng)
+    for s in sorted(count):
+        g.wait_ge(T.sem[s], count[s])

@@ -18,20 +18,19 @@ def _scratch():
     sb("bfloat16", 2048, "et")
     sb("bfloat16", 1408, "fg")
     sb("bfloat16", 1024, "x0 z xt ct pt")
-    sb("bfloat16", 512, "u0 v0 ta tb ft sl")
+    sb("bfloat16", 512, "zero u0 v0 ta tb ft sl")
     sb("bfloat16", 272, "hp0 hp1 hp2 hp3")
-    sb("bfloat16", 256, "row msk rsI rs lic1 lic2 d wa wb iv z320 z321 z322 z323 tt0 tt1 tt2 tt3")
+    sb("bfloat16", 256, "row msk rsI rs lic1 lic2 tbm d wa wb iv z320 z321 z322 z323 tt0 tt1 tt2 tt3")
     sb("bfloat16", 128, "ones neg ident nb nb2 rr rr2")
     sb("uint16", 16, "mo0 mo1 mo2 inv0 inv1 inv2 pos off0 off1 off2 off3")
     sb("uint16", 6, "slot0 slot1 slot2 land0 land1 land2")
     sb("uint16", 8, "pick8")
     sb("int32", 8, "pick8i")
     sb("int32", 16, "mi0 mi1 mi2 ipI")
-    sb("int32", 256, "mskI")
     sb("float32", 16, "ic leg m16")
     sb("float32", 32, "m32")
     sb("float32", 48, "mf")
-    sb("float32", 64, "zz cum pp")
+    sb("float32", 64, "cum pp")
     sb("float32", 192, "ll")
     sb("float32", 256, "wrow yb")
     for n in "k0 k1 k2 k3 b0 b1 b2 b3".split():
@@ -40,7 +39,7 @@ def _scratch():
 
 
 SCRATCH = _scratch()
-LOADS = ["u", "xa", "xb", "v", "wc", "ws", "m0", "m1", "m2"]
+LOADS = ["u", "xa", "xb", "v", "wc", "ws", "m0", "m1", "m2", "inv"]
 SEMAPHORES = ["sV", "sT", "sA", "sG", "loc", "st", "st2"] + ["ld_" + n for n in LOADS] + ["ah0", "ah1", "ah2", "al0", "al1", "al2"]
 
 
@@ -128,16 +127,20 @@ def rank_program(g, core, T, topo):
     def dma(q, out, in_, sem, r="", w=""):
         op(q, lambda: queues[q].dma_start(out, in_), r.split(), w.split(), sem, 16)
 
-    def wrapped(src, n, tok):
-        V(scan(T.wa[:, 0:n], src, T.msk[:, 0:n], BIG, A.min, A.max), tok + " msk", "wa")
-        V(scan(T.wb[:, 0:n], T.rs[:, 0:n], T.wa[:, 0:n], BIG, A.max, A.min), "wa rs", "wb")
+    def own(src, n, tok, out="wa"):
+        V(scan(T[out][:, 0:n], src, T.msk[:, 0:n], BIG, A.min, A.max), tok + " msk", out)
+
+    def wrap(src, n, tok):
+        V(scan(T.wb[:, 0:n], T.rs[:, 0:n], src, BIG, A.max, A.min), tok + " rs", "wb")
 
     def const(name, pat, base, ch, in_=None, cmp=None, fv=None):
+        out = T[name][:]
         if in_ is None:
             small = SCRATCH[name][2] != "int32"
-            op("G", lambda: g.iota(T[name][:], pat, base, ch, allow_small_or_imprecise_dtypes=small), [], [name])
+            op("G", lambda: g.iota(out, pat, base, ch, allow_small_or_imprecise_dtypes=small), [], [name])
         else:
-            op("G", lambda: g.affine_select(T[name][:], T[in_][:], pat, cmp, fv, base, ch), [in_], [name])
+            src = T[in_][:, 0:SCRATCH[name][1][1]]
+            op("G", lambda: g.affine_select(out, src, pat, cmp, fv, base, ch), [in_], [name])
 
     dma("S", T.u0[:], T.u[:], "ld_u", "", "u0")
     dma("A", T.x0[:, 0:512], T.x[:, 0:512], "ld_xa", "", "x0a")
@@ -151,73 +154,57 @@ def rank_program(g, core, T, topo):
         dma("S", T["mi%d" % t][128 - n:128, :], T.m[0:n, :], "ld_m%d" % t, "", "mi%d" % t)
     dma("S", T.v0[:], T.v[:], "ld_v", "", "v0")
 
+    V(fill(T.zero[:], 0.0), "", "zero")
     V(fill(T.ones[:], 1.0), "", "ones")
     V(fill(T.neg[:], -1.0), "", "neg")
     const("pick8i", [[16, 8]], 0, 0)
     const("ident", [[-1, 128]], 0, 1, "ones", A.is_equal, 0.0)
-    const("mskI", [[1, 256]], 128, -1)
-    const("rsI", [[0, 16], [1, 16]], 0, 0)
     const("nb", [[-16, 8], [0, 16]], 0, 1, "neg", A.is_ge, 0.0)
     const("nb2", [[16, 8], [0, 16]], 15, -1, "nb", A.is_ge, 0.0)
     const("rr", [[-1, 128]], 0, 1, "nb2", A.is_gt, 0.0)
     const("rr2", [[-1, 128]], 0, 1, "rr", A.not_equal, -1024.0)
-    const("row", [[1, 256]], 0, 0)
     const("ipI", [[0, 16]], 0, 1)
     const("ic", [[16, 16]], 0, 0)
+    const("rsI", [[0, 16], [1, 16]], 0, 0)
+    const("rs", [[0, 16], [1, 16]], 0, 0, "zero", A.not_equal, BIG)
+    const("row", [[1, 256]], 0, 0)
+    for b in range(4):
+        act(T.et[:, 512 * b:512 * b + 512], T.zero[:], "zero", "et%d" % b)
     V(fill(T.ct[:], 0.0), "", "ct")
     V(fill(T.ct[:, 0:512:4], 0.0625), "", "ct")
     V(fill(T.ct[:, 514:1024:4], 0.0625), "", "ct")
     quant("c", T.ct[:], 0, 256, "ct", "qc")
-    V(fill(T.ta[:], 0.0), "", "ta")
     V(cp(T.pick8[:], T.pick8i[:]), "pick8i", "pick8")
-    V(fill(T.et[:], 0.0), "", "et")
+    V(fill(T.ta[:], 0.0), "", "ta")
+    V(fill(T.tb[:], 0.0), "", "tb")
     quant("u", T.u0[:], 0, 128, "u0", "qu")
     V(cp(T.qu16[:, 0:128].bitcast(dt.uint32), T.qu[:, 0:128].bitcast(dt.uint32).indirect(T.pick8[:, 0:8])), "qu pick8", "qu16")
-    V(cp(T.su16[:, 0:128], T.su[:, 0:128].indirect(T.pick8[:, 0:8])), "qu pick8", "su16")
+    act(T.su16[:, 0:128], T.su[:, 0:128].indirect(T.pick8[:, 0:8]), "qu pick8", "su16")
+    for b in range(4):
+        act(T.et[:, 512 * b + b:512 * b + 512:4], T.ident[:], "ident", "et%d" % b)
+    for h in (0, 1):
+        act(T.pt[:, 512 * h:512 * h + 512], T.zero[:], "zero", "pt%d" % h)
+    act(T.pt[:, 0:512:4], T.rr2[:], "rr2", "pt0")
+    act(T.pt[:, 512:1024:4], T.nb2[:], "nb2", "pt1", scale=-1.0)
 
-    def late_constants():
-        for b in range(4):
-            V(cp(T.et[:, 512 * b + b:512 * b + 512:4], T.ident[:]), "ident et", "et%d" % b)
-        quant("e", T.et[:], 0, 512, "et et0 et1 et2 et3", "qe")
-        V(fill(T.tb[:], 0.0), "", "tb")
-        V(cp(T.mo0[:], T.mi0[:]), "mi0", "mo0")
-
-    def later_constants():
-        V(ts(T.mskI[:], T.mskI[:], 15, None, A.bitwise_and), "mskI", "mskI")
-        V(ts(T.msk[:], T.mskI[:], 0.0, BIG, A.is_gt, A.mult), "mskI", "msk")
-        V(ts(T.rs[:], T.rsI[:], 0.0, BIG, A.is_equal, A.mult), "rsI", "rs")
-        V(fill(T.ft[:], 0.0), "", "ft")
-        V(fill(T.pt[:], 0.0), "", "pt")
-        V(cp(T.pt[:, 0:512:4], T.rr2[:]), "rr2", "pt")
-        V(ts(T.pt[:, 512:1024:4], T.nb2[:], -1.0, None, A.mult), "nb2", "pt")
-        quant("p", T.pt[:], 0, 256, "pt", "qp")
-        V(fill(T.zz[:], 0.0), "", "zz")
-        V(ts(T.ipI[:], T.ipI[:], 15, None, A.bitwise_and), "ipI", "ipI")
-        V(tt(T.leg[:], T.ipI[:], T.ic[:], A.add), "ipI ic", "leg")
-        V(ts(T.pp[:, 48:64], T.leg[:], -767.0, None, A.add), "leg", "pc")
-        V(cp(T.mf[:, 0:16], T.mi0[:]), "mi0", "mf0")
-
-    def last_constants():
-        for b in range(4):
-            V(fill(T["hp%d" % b][:, 256:272], 0.0), "", "hz%d" % b)
-        for t in (1, 2):
-            V(cp(T["mo%d" % t][:], T["mi%d" % t][:]), "mi%d" % t, "mo%d" % t)
-            V(cp(T.mf[:, 16 * t:16 * t + 16], T["mi%d" % t][:]), "mi%d" % t, "mf%d" % t)
-        quant("v", T.v0[:], 0, 128, "v0", "qv")
-
+    xs = ["xs%d%d" % (b, h) for h in (0, 1) for b in range(4)]
     even = slice(0, 512, 2)
-    xs = "xs0 xs1 xs2 xs3"
+    L = [T.ll[:, 16 * k:16 * k + 16] for k in range(12)]
+    F3, F2, F1, F4 = [T.ft[:, 64 * k:64 * k + 64:4] for k in range(4)]
+
+    def quant_x(h, src, r):
+        quant("x", src[:, 512 * h:512 * h + 512], 128 * h, 128 * h + 128, r, "qx%d" % h)
+
+    quant_x(0, T.x0, "x0a")
+    quant_x(1, T.x0, "x0b")
     for t in range(R):
         mo = T["mo%d" % t][:, 0:16]
         mot = " mo%d" % t
-        X = T.xt if t else T.x0
-        quant("x", X[:, 0:512], 0, 128, xs if t else "x0a", "qxa")
-        quant("x", X[:, 512:1024], 128, 256, xs if t else "x0b", "qxb")
-        mm("k0", "u16", 0, "x", 0, 128, "qu16 su16 qxa")
-        mm("k1", "u16", 0, "x", 128, 256, "qu16 su16 qxb")
+        mm("k0", "u16", 0, "x", 0, 128, "qu16 su16 qx0")
+        mm("k1", "u16", 0, "x", 128, 256, "qu16 su16 qx1")
 
         def unpack(b):
-            mm("b%d" % b, "e", 128 * b, "x", 0, 256, "qe qxa qxb")
+            mm("b%d" % b, "e", 128 * b, "x", 0, 256, "qe qx0 qx1")
             act(T.fg[:, b:1024:4], T["b%d" % b][:, 0:256], "b%d" % b, "f%d" % b)
         if t:
             unpack(0)
@@ -227,10 +214,16 @@ def rank_program(g, core, T, topo):
         mm("k2", "c", 0, "ta", 0, 128, "qc qta")
         mm("k3", "c", 128, "ta", 0, 128, "qc qta")
         if t == 0:
-            late_constants()
+            V(cp(T.mo0[:], T.mi0[:]), "mi0", "mo0")
+            quant("e", T.et[:], 0, 512, "et0 et1 et2 et3", "qe")
             unpack(0)
         for b in (1, 2, 3):
             unpack(b)
+        if t == 0:
+            act(T.ft[:], T.zero[:], "zero", "ft")
+            for b in range(4):
+                act(T["hp%d" % b][:, 256:272], T.zero[:, 0:16], "zero", "hz%d" % b)
+        V(fill(T.sl[:, 0:96], 256.0), "", "sl")
         V(ts(T.lic1[:, 0:256:2], T.k2[:, 0:128], 5.5, 1.125, A.is_ge, A.mult), "k2", "lic1a")
         V(ts(T.lic1[:, 1:256:2], T.k3[:, 0:128], 5.5, 1.125, A.is_ge, A.mult), "k3", "lic1b")
         V(tt(T.tb[:, even], T.lic1[:, 0:256].indirect(mo), T.ta[:, even], A.max), "lic1a lic1b ta0 ta1 tb" + mot, "tbv")
@@ -238,39 +231,45 @@ def rank_program(g, core, T, topo):
         mm("k2", "c", 0, "tb", 0, 128, "qc qtb")
         mm("k3", "c", 128, "tb", 0, 128, "qc qtb")
         if t == 0:
-            later_constants()
-        V(ts(T.lic2[:, 0:256:2], T.k2[:, 0:128], 5.5, 0.875, A.is_ge, A.max), "k2", "lic2a")
-        V(ts(T.lic2[:, 1:256:2], T.k3[:, 0:128], 5.5, 0.875, A.is_ge, A.max), "k3", "lic2b")
-        V(tt(T.d[:], T.lic2[:, 0:256].indirect(mo), T.tb[:, even], A.max), "lic2a lic2b tbv" + mot, "d")
-        wrapped(T.d[:], 256, "d")
-        for k, code in enumerate((1.0, 1.125, 1.25, 0.875)):
-            V(ts(T.ft[:, 64 * k:64 * k + 64:4], T.wb[:, 15:256:16], code, None, A.is_equal), "wb ft", "ft%d" % k)
-        quant("ft", T.ft[:], 0, 128, "ft ft0 ft1 ft2 ft3", "qft")
-        mm("k1", "p", 128, "ft", 0, 128, "qp qft")
-        mm("k0", "p", 0, "ft", 0, 128, "qp qft")
+            V(ts(T.ipI[:], T.ipI[:], 15, None, A.bitwise_and), "ipI", "ipI")
+            V(tt(T.leg[:], T.ipI[:], T.ic[:], A.add), "ipI ic", "leg")
+            V(ts(T.msk[:], T.rsI[:], T.leg[:, 0:1], BIG, A.not_equal, A.mult), "rsI leg", "msk")
+        own(T.tb[:, even], 256, "tbv", "tbm")
         quant("f%d" % t, T.fg[:, 0:1024], 0, 256, "f0 f1 f2 f3", "qf")
         order("G", [writer["qf"]])
         g.remote_dma(T["qh%d" % t][:].bitcast(dt.uint8), T["qf%d" % t][:].bitcast(dt.uint8), T.sem["ah%d" % t], T.sem.loc, pid, rid, mask)
         g.remote_dma(T["sh%d" % t][:], T["sf%d" % t][:], T.sem["ah%d" % t], T.sem.loc, pid, rid, mask)
-        V(fill(T.sl[:, 0:96], 256.0), "", "sl")
-        V(scan(T.cum[:], T.k1[:, 0:64], T.zz[:], 0.0, A.add, A.add), "k1 zz", "cum")
+        V(ts(T.lic2[:, 0:256:2], T.k2[:, 0:128], 5.5, 0.875, A.is_ge, A.max), "k2", "lic2a")
+        V(ts(T.lic2[:, 1:256:2], T.k3[:, 0:128], 5.5, 0.875, A.is_ge, A.max), "k3", "lic2b")
+        V(tt(T.wa[:], T.lic2[:, 0:256].indirect(mo), T.tbm[:], A.max), "lic2a lic2b tbm" + mot, "wa")
+        wrap(T.wa[:], 256, "wa")
+        for k, code in enumerate((1.0, 1.125, 1.25, 0.875)):
+            V(ts(T.ft[:, 64 * k:64 * k + 64:4], T.wb[:, 15:256:16], code, None, A.is_equal), "wb ft", "ft%d" % k)
+        quant("ft", T.ft[:], 0, 128, "ft ft0 ft1 ft2 ft3", "qft")
+        if t == 0:
+            quant("p", T.pt[:], 0, 256, "pt0 pt1", "qp")
+            V(ts(T.pp[:, 48:64], T.leg[:], -767.0, None, A.add), "leg", "pc")
+            for k in range(R):
+                V(cp(T.mf[:, 16 * k:16 * k + 16], T["mi%d" % k][:]), "mi%d" % k, "mf%d" % k)
+        mm("k1", "p", 128, "ft", 0, 128, "qp qft")
+        mm("k0", "p", 0, "ft", 0, 128, "qp qft")
+        V(tt(L[0], F1, T.leg[:], A.mult), "ft2 leg", "l0")
+        V(tt(L[1], F2, F3, A.add), "ft0 ft1", "l1")
+        V(tt(L[2], L[1], T.mf[:, 16 * t:16 * t + 16], A.mult), "l1 mf%d" % t, "l2")
+        V(scan(T.cum[:], T.k1[:, 0:64], T.zero[:, 0:64], 0.0, A.add, A.add), "k1 zero", "cum")
         V(tt(T.pp[:, 0:48], T.cum[:, 0:48], T.k0[:, 0:48], A.add), "cum k0", "pp")
         V(tt(T.m32[:], T.pp[:, 0:32], T.pp[:, 32:64], A.min), "pp pc", "m32")
         V(tt(T.m16[:], T.m32[:, 0:16], T.m32[:, 16:32], A.min), "m32", "m16")
         V(ts(T.pos[:], T.m16[:], 1023.0, None, A.add), "m16", "pos")
         V(cp(T.sl[:, 0:512].indirect(T.pos[:, 0:16]), T.row[:, 0:256]), "pos row", "sl")
-        wrapped(T.sl[:, 0:96], 96, "sl")
+        own(T.sl[:, 0:96], 96, "sl")
+        wrap(T.wa[:, 0:96], 96, "wa")
         V(cp(T["slot%d" % t][:, 0:6], T.wb[:, 15:96:16]), "wb", "slot")
         order("G", [writer["slot"]])
         g.remote_dma(T["land%d" % t][:], T["slot%d" % t][:], T.sem["al%d" % t], T.sem.loc, pid, rid, mask)
-        L = [T.ll[:, 16 * k:16 * k + 16] for k in range(12)]
-        F3, F2, F1, F4 = [T.ft[:, 64 * k:64 * k + 64:4] for k in range(4)]
-        V(tt(L[0], F1, T.leg[:], A.mult), "ft2 leg", "l0")
-        V(tt(L[1], F2, F3, A.add), "ft0 ft1", "l1")
         V(tt(L[3], T.cum[:, 48:64], T.k0[:, 48:64], A.add), "cum k0", "l3")
-        V(tt(L[2], L[1], T.mf[:, 16 * t:16 * t + 16], A.mult), "l1 mf%d" % t, "l2")
-        V(ts(L[4], L[3], T.cum[:, 47:48], 1279.0, A.subtract, A.add), "l3 cum", "l4")
         V(tt(L[5], L[0], L[2], A.add), "l0 l2", "l5")
+        V(ts(L[4], L[3], T.cum[:, 47:48], 1279.0, A.subtract, A.add), "l3 cum", "l4")
         V(ts(L[6], L[4], 352.0, -96.0, A.is_ge, A.mult), "l4", "l6")
         V(ts(L[7], L[4], 448.0, -96.0, A.is_ge, A.mult), "l4", "l7")
         V(tt(L[8], L[4], L[6], A.add), "l4 l6", "l8")
@@ -280,18 +279,28 @@ def rank_program(g, core, T, topo):
         for b in range(4):
             V(ts(T["off%d" % b][:], L[11], 4.0, float(b), A.mult, A.add), "l11", "off%d" % b)
         if t == 0:
-            last_constants()
-        V(cp(T.iv[:, 0:256].indirect(mo), T.row[:, 0:256]), "row" + mot, "iv")
-        wrapped(T.iv[:], 256, "iv")
-        V(cp(T["inv%d" % t][:, 0:16], T.wb[:, 15:256:16]), "wb", "inv")
+            V(cp(T.iv[:, 0:256].indirect(mo), T.row[:, 0:256]), "row" + mot, "iv")
+            own(T.iv[:], 256, "iv")
+            wrap(T.wa[:], 256, "wa")
+            V(cp(T.inv0[:, 0:16], T.wb[:, 15:256:16]), "wb", "inv0")
+            for k in (1, 2):
+                n = 16 * k
+                V(cp(T["mo%d" % k][:], T["mi%d" % k][:]), "mi%d" % k, "mo%d" % k)
+                dma("S", T["inv%d" % k][0:128 - n, :], T.inv0[n:128, :], "ld_inv", "inv0", "inv%da" % k)
+                dma("S", T["inv%d" % k][128 - n:128, :], T.inv0[0:n, :], "ld_inv", "inv0", "inv%d" % k)
+            writer["inv1"] = writer["inv2"]
+        elif t == 1:
+            quant("v", T.v0[:], 0, 128, "v0", "qv")
         if t == R - 1:
-            act(T.wrow[:], T.d[:], "d", "wrow", bias=11.0, scale=-8.0)
-            dma("S", T.wv[:], T.wrow[0:128:16, :], "st", "wrow")
+            V(tt(T.d[:], T.lic2[:, 0:256].indirect(mo), T.tb[:, even], A.max), "lic2a lic2b tbv" + mot, "d")
         writer["hh"] = ("ah%d" % t, 2 * neng, {})
         writer["land"] = ("al%d" % t, neng, {})
         for b in range(4):
             mm("b%d" % b, "e", 128 * b, "h%d" % t, 0, 256, "qe hh")
             act(T["hp%d" % b][:, 0:256], T["b%d" % b][:, 0:256], "b%d" % b, "hp%d" % b)
+        if t == R - 1:
+            act(T.wrow[:], T.d[:], "d", "wrow", bias=11.0, scale=-8.0)
+            dma("S", T.wv[:], T.wrow[0:128:16, :], "st", "wrow")
         for b in (0, 2, 1, 3):
             src, out = T["hp%d" % b][:, 0:272].indirect(T["land%d" % t][:, 0:6]), T.fg[:, 1024 + b:1408:4]
             r, w = "hp%d hz%d land" % (b, b), "g%d" % b
@@ -315,17 +324,20 @@ def rank_program(g, core, T, topo):
             act(T["z32%d" % b][:], T.z[:, b:1024:4], "z%d" % b, "z32%d" % b, scale=32.0)
         for b in range(4):
             V(tt(T["tt%d" % b][:], T["b%d" % b][:, 0:256], T["z32%d" % b][:], A.add), "b%d z32%d" % (b, b), "tt%d" % b)
-            src, out = T["tt%d" % b][:, 0:256].indirect(T["inv%d" % t][:, 0:16]), T.xt[:, b:1024:4]
-            if b == 3:
-                V(ts(out, src, 0.03125, None, A.mult), "inv tt%d" % b, "xs%d" % b)
-            else:
-                act(out, src, "inv tt%d" % b, "xs%d" % b, scale=0.03125)
-    for h, k in ((0, "qxa"), (1, "qxb")):
-        quant("x", T.xt[:, 512 * h:512 * h + 512], 128 * h, 128 * h + 128, xs, k)
-        dma("S", T.oc[:, 512 * h:512 * h + 512], T.qx[:, 128 * h:128 * h + 128].bitcast(dt.uint8), "st", k)
-        mm("k%d" % h, "v", 0, "x", 128 * h, 128 * h + 128, "qv " + k)
+        for h in (0, 1):
+            for b in range(4):
+                src = T["tt%d" % b][:, 0:256].indirect(T["inv%d" % t][:, 8 * h:8 * h + 8])
+                out, r, w = T.xt[:, 512 * h + b:512 * h + 512:4], "inv%d tt%d" % (t, b), "xs%d%d" % (b, h)
+                if b == 3:
+                    V(ts(out, src, 0.03125, None, A.mult), r, w)
+                else:
+                    act(out, src, r, w, scale=0.03125)
+            quant_x(h, T.xt, " ".join(xs[4 * h:4 * h + 4]))
+    for h in (0, 1):
+        dma("S", T.oc[:, 512 * h:512 * h + 512], T.qx[:, 128 * h:128 * h + 128].bitcast(dt.uint8), "st", "qx%d" % h)
+        mm("k%d" % h, "v", 0, "x", 128 * h, 128 * h + 128, "qv qx%d" % h)
     for k in range(4):
-        dma("A", T.osc[4 * k:4 * k + 4, :], T.sx[32 * k:32 * k + 4, :], "st2", "qxa qxb")
+        dma("A", T.osc[4 * k:4 * k + 4, :], T.sx[32 * k:32 * k + 4, :], "st2", "qx0 qx1")
     for h in (0, 1):
         V(cp(T.yb[:, 128 * h:128 * h + 128], T["k%d" % h][:, 0:128]), "k%d" % h, "yb%d" % h)
         dma("S", T.y[:, 128 * h:128 * h + 128], T.yb[:, 128 * h:128 * h + 128], "st", "yb%d" % h)

from concourse.mybir import dt, AluOpType, ActivationFunctionType

R = 3
BIG = 512.0


def _scratch():
    s = {}

    def sb(d, w, names):
        for n in names.split():
            s[n] = ("sbuf", [128, w], d)

    for w, names in ((128, "u u16 v ta tb ft"), (256, "x c p z f0 f1 f2 h0 h1 h2"), (512, "w e")):
        for n in names.split():
            s["q" + n] = ("sbuf", [128, w], "float8_e4m3fn_x4")
            s["s" + n] = ("sbuf", [128, w], "uint8")
    sb("bfloat16", 2048, "et")
    sb("bfloat16", 1408, "fg")
    sb("bfloat16", 1024, "x0 z xt ct pt")
    sb("bfloat16", 512, "zero u0 v0 ta tb ft sl")
    sb("bfloat16", 272, "hp0 hp1 hp2 hp3")
    sb("bfloat16", 256, "row msk rsI rs lic1 lic2 tbm d wa wb iv z320 z321 z322 z323 tt0 tt1 tt2 tt3")
    sb("bfloat16", 128, "ones neg ident nb nb2 rr rr2")
    sb("uint16", 16, "mo0 mo1 mo2 inv0 inv1 inv2 pos off0 off1 off2 off3")
    sb("uint16", 6, "slot0 slot1 slot2 land0 land1 land2")
    sb("uint16", 8, "pick8")
    sb("int32", 8, "pick8i")
    sb("int32", 16, "mi0 mi1 mi2 ipI")
    sb("float32", 16, "ic leg m16")
    sb("float32", 32, "m32")
    sb("float32", 48, "mf")
    sb("float32", 64, "cum pp")
    sb("float32", 192, "ll")
    sb("float32", 256, "wrow yb")
    for n in "k0 k1 k2 k3 b0 b1 b2 b3".split():
        s[n] = ("psum", [128, 512], "float32")
    return s


SCRATCH = _scratch()
LOADS = ["u", "xa", "xb", "v", "wc", "ws", "m0", "m1", "m2", "inv"]
SEMAPHORES = ["sV", "sT", "sA", "sG", "loc", "st", "st2"] + ["ld_" + n for n in LOADS] + ["ah0", "ah1", "ah2", "al0", "al1", "al2"]


def rank_program(g, core, T, topo):
    rank = T.rank_of(core)
    if rank is None:
        return
    A = AluOpType
    COPY = ActivationFunctionType.Copy
    nxt = T.cores[(rank + 1) % len(T.cores)]
    rid, pid = topo.addr(nxt)[0], topo.addr(nxt)[1]
    mask, neng = topo.mask(core, nxt), len(topo.engines(core, nxt))
    queues = {"V": g.vector, "T": g.tensor, "A": g.scalar, "G": g, "S": g.sync}
    known = {q: {} for q in queues}
    count, writer, readers = {}, {}, {}

    def order(q, need):
        best = {}
        for e in need:
            if known[q].get(e[0], 0) < e[1] and (e[0] not in best or best[e[0]][1] < e[1]):
                best[e[0]] = e
        for s in list(best):
            if any(o != s and best[o][2].get(s, 0) >= best[s][1] for o in best):
                del best[s]
        for s in best:
            _, v, c = best[s]
            queues[q].wait_ge(T.sem[s], v)
            for k in c:
                known[q][k] = max(known[q].get(k, 0), c[k])
            known[q][s] = max(known[q].get(s, 0), v)

    def op(q, fn, r=(), w=(), sem=None, inc=1):
        need = []
        for k in r:
            if k in writer:
                need.append(writer[k])
        for k in w:
            if k in writer:
                need.append(writer[k])
            need += [e for qq, e in readers.get(k, {}).items() if qq != q]
        order(q, need)
        i = fn()
        s = sem or "s" + q
        i.then_inc(T.sem[s], inc)
        count[s] = count.get(s, 0) + inc
        c = dict(known[q])
        c[s] = count[s]
        e = (s, count[s], c)
        for k in r:
            readers.setdefault(k, {})[q] = e
        for k in w:
            writer[k] = e
            readers[k] = {}

    def V(fn, r="", w=""):
        op("V", fn, r.split(), w.split())

    def act(out, in_, r, w, **kw):
        op("A", lambda: g.scalar.activation(out, in_, COPY, **kw), r.split(), w.split())

    def ts(out, in0, s1, s2, op0, op1=None):
        if op1 is None:
            return lambda: g.vector.tensor_scalar(out, in0, s1, None, op0)
        return lambda: g.vector.tensor_scalar(out, in0, s1, s2, op0, op1)

    def tt(out, a, b, o):
        return lambda: g.vector.tensor_tensor(out, a, b, o)

    def cp(out, a):
        return lambda: g.vector.tensor_copy(out, a)

    def fill(ap, v):
        return lambda: g.vector.memset(ap, v)

    def scan(out, a, b, init, o0, o1):
        return lambda: g.vector.tensor_tensor_scan(out, a, b, init, o0, o1)

    def quant(n, src, a, b, r, tok):
        V(lambda: g.vector.quantize_mx(T["q" + n][:, a:b], T["s" + n][:, a:b], src), r, tok)

    def mm(bank, ln, la, rn, ra, rb, r):
        op("T", lambda: g.tensor.matmul_mx(T[bank][:, 0:rb - ra], T["q" + ln][:, la:la + 128], T["s" + ln][:, la:la + 128],
                                           T["q" + rn][:, ra:rb], T["s" + rn][:, ra:rb], True, True), r.split(), [bank])

    def dma(q, out, in_, sem, r="", w=""):
        op(q, lambda: queues[q].dma_start(out, in_), r.split(), w.split(), sem, 16)

    def own(src, n, tok, out="wa"):
        V(scan(T[out][:, 0:n], src, T.msk[:, 0:n], BIG, A.min, A.max), tok + " msk", out)

    def wrap(src, n, tok):
        V(scan(T.wb[:, 0:n], T.rs[:, 0:n], src, BIG, A.max, A.min), tok + " rs", "wb")

    def const(name, pat, base, ch, in_=None, cmp=None, fv=None):
        out = T[name][:]
        if in_ is None:
            small = SCRATCH[name][2] != "int32"
            op("G", lambda: g.iota(out, pat, base, ch, allow_small_or_imprecise_dtypes=small), [], [name])
        else:
            src = T[in_][:, 0:SCRATCH[name][1][1]]
            op("G", lambda: g.affine_select(out, src, pat, cmp, fv, base, ch), [in_], [name])

    dma("S", T.u0[:], T.u[:], "ld_u", "", "u0")
    dma("A", T.x0[:, 0:512], T.x[:, 0:512], "ld_xa", "", "x0a")
    dma("S", T.mi0[:], T.m[:], "ld_m0", "", "mi0")
    dma("A", T.x0[:, 512:1024], T.x[:, 512:1024], "ld_xb", "", "x0b")
    dma("S", T.qw[:].bitcast(dt.uint8), T.wc[:], "ld_wc", "", "qw")
    dma("S", T.sw[:], T.ws[:], "ld_ws", "", "sw")
    for t in (1, 2):
        n = 16 * t
        dma("S", T["mi%d" % t][0:128 - n, :], T.m[n:128, :], "ld_m%d" % t, "", "mi%da" % t)
        dma("S", T["mi%d" % t][128 - n:128, :], T.m[0:n, :], "ld_m%d" % t, "", "mi%d" % t)
    dma("S", T.v0[:], T.v[:], "ld_v", "", "v0")

    V(fill(T.zero[:], 0.0), "", "zero")
    V(fill(T.ones[:], 1.0), "", "ones")
    V(fill(T.neg[:], -1.0), "", "neg")
    const("pick8i", [[16, 8]], 0, 0)
    const("ident", [[-1, 128]], 0, 1, "ones", A.is_equal, 0.0)
    const("nb", [[-16, 8], [0, 16]], 0, 1, "neg", A.is_ge, 0.0)
    const("nb2", [[16, 8], [0, 16]], 15, -1, "nb", A.is_ge, 0.0)
    const("rr", [[-1, 128]], 0, 1, "nb2", A.is_gt, 0.0)
    const("rr2", [[-1, 128]], 0, 1, "rr", A.not_equal, -1024.0)
    const("ipI", [[0, 16]], 0, 1)
    const("ic", [[16, 16]], 0, 0)
    const("rsI", [[0, 16], [1, 16]], 0, 0)
    const("rs", [[0, 16], [1, 16]], 0, 0, "zero", A.not_equal, BIG)
    const("row", [[1, 256]], 0, 0)
    for b in range(4):
        act(T.et[:, 512 * b:512 * b + 512], T.zero[:], "zero", "et%d" % b)
    V(fill(T.ct[:], 0.0), "", "ct")
    V(fill(T.ct[:, 0:512:4], 0.0625), "", "ct")
    V(fill(T.ct[:, 514:1024:4], 0.0625), "", "ct")
    quant("c", T.ct[:], 0, 256, "ct", "qc")
    V(cp(T.pick8[:], T.pick8i[:]), "pick8i", "pick8")
    V(fill(T.ta[:], 0.0), "", "ta")
    V(fill(T.tb[:], 0.0), "", "tb")
    quant("u", T.u0[:], 0, 128, "u0", "qu")
    V(cp(T.qu16[:, 0:128].bitcast(dt.uint32), T.qu[:, 0:128].bitcast(dt.uint32).indirect(T.pick8[:, 0:8])), "qu pick8", "qu16")
    act(T.su16[:, 0:128], T.su[:, 0:128].indirect(T.pick8[:, 0:8]), "qu pick8", "su16")
    for b in range(4):
        act(T.et[:, 512 * b + b:512 * b + 512:4], T.ident[:], "ident", "et%d" % b)
    for h in (0, 1):
        act(T.pt[:, 512 * h:512 * h + 512], T.zero[:], "zero", "pt%d" % h)
    act(T.pt[:, 0:512:4], T.rr2[:], "rr2", "pt0")
    act(T.pt[:, 512:1024:4], T.nb2[:], "nb2", "pt1", scale=-1.0)

    xs = ["xs%d%d" % (b, h) for h in (0, 1) for b in range(4)]
    even = slice(0, 512, 2)
    L = [T.ll[:, 16 * k:16 * k + 16] for k in range(12)]
    F3, F2, F1, F4 = [T.ft[:, 64 * k:64 * k + 64:4] for k in range(4)]

    def quant_x(h, src, r):
        quant("x", src[:, 512 * h:512 * h + 512], 128 * h, 128 * h + 128, r, "qx%d" % h)

    quant_x(0, T.x0, "x0a")
    quant_x(1, T.x0, "x0b")
    for t in range(R):
        mo = T["mo%d" % t][:, 0:16]
        mot = " mo%d" % t
        mm("k0", "u16", 0, "x", 0, 128, "qu16 su16 qx0")
        mm("k1", "u16", 0, "x", 128, 256, "qu16 su16 qx1")

        def unpack(b):
            mm("b%d" % b, "e", 128 * b, "x", 0, 256, "qe qx0 qx1")
            act(T.fg[:, b:1024:4], T["b%d" % b][:, 0:256], "b%d" % b, "f%d" % b)
        if t:
            unpack(0)
        for h in (0, 1):
            V(ts(T.ta[:, 256 * h:256 * h + 256:2], T["k%d" % h][:, 0:128], 0.0, 1.25, A.is_gt, A.mult), "ta k%d" % h, "ta%d" % h)
        quant("ta", T.ta[:], 0, 128, "ta ta0 ta1", "qta")
        mm("k2", "c", 0, "ta", 0, 128, "qc qta")
        mm("k3", "c", 128, "ta", 0, 128, "qc qta")
        if t == 0:
            V(cp(T.mo0[:], T.mi0[:]), "mi0", "mo0")
            quant("e", T.et[:], 0, 512, "et0 et1 et2 et3", "qe")
            unpack(0)
        for b in (1, 2, 3):
            unpack(b)
        if t == 0:
            act(T.ft[:], T.zero[:], "zero", "ft")
            for b in range(4):
                act(T["hp%d" % b][:, 256:272], T.zero[:, 0:16], "zero", "hz%d" % b)
        V(fill(T.sl[:, 0:96], 256.0), "", "sl")
        V(ts(T.lic1[:, 0:256:2], T.k2[:, 0:128], 5.5, 1.125, A.is_ge, A.mult), "k2", "lic1a")
        V(ts(T.lic1[:, 1:256:2], T.k3[:, 0:128], 5.5, 1.125, A.is_ge, A.mult), "k3", "lic1b")
        V(tt(T.tb[:, even], T.lic1[:, 0:256].indirect(mo), T.ta[:, even], A.max), "lic1a lic1b ta0 ta1 tb" + mot, "tbv")
        quant("tb", T.tb[:], 0, 128, "tb tbv", "qtb")
        mm("k2", "c", 0, "tb", 0, 128, "qc qtb")
        mm("k3", "c", 128, "tb", 0, 128, "qc qtb")
        if t == 0:
            V(ts(T.ipI[:], T.ipI[:], 15, None, A.bitwise_and), "ipI", "ipI")
            V(tt(T.leg[:], T.ipI[:], T.ic[:], A.add), "ipI ic", "leg")
            V(ts(T.msk[:], T.rsI[:], T.leg[:, 0:1], BIG, A.not_equal, A.mult), "rsI leg", "msk")
        own(T.tb[:, even], 256, "tbv", "tbm")
        quant("f%d" % t, T.fg[:, 0:1024], 0, 256, "f0 f1 f2 f3", "qf")
        order("G", [writer["qf"]])
        g.remote_dma(T["qh%d" % t][:].bitcast(dt.uint8), T["qf%d" % t][:].bitcast(dt.uint8), T.sem["ah%d" % t], T.sem.loc, pid, rid, mask)
        g.remote_dma(T["sh%d" % t][:], T["sf%d" % t][:], T.sem["ah%d" % t], T.sem.loc, pid, rid, mask)
        V(ts(T.lic2[:, 0:256:2], T.k2[:, 0:128], 5.5, 0.875, A.is_ge, A.max), "k2", "lic2a")
        V(ts(T.lic2[:, 1:256:2], T.k3[:, 0:128], 5.5, 0.875, A.is_ge, A.max), "k3", "lic2b")
        V(tt(T.wa[:], T.lic2[:, 0:256].indirect(mo), T.tbm[:], A.max), "lic2a lic2b tbm" + mot, "wa")
        wrap(T.wa[:], 256, "wa")
        for k, code in enumerate((1.0, 1.125, 1.25, 0.875)):
            V(ts(T.ft[:, 64 * k:64 * k + 64:4], T.wb[:, 15:256:16], code, None, A.is_equal), "wb ft", "ft%d" % k)
        quant("ft", T.ft[:], 0, 128, "ft ft0 ft1 ft2 ft3", "qft")
        if t == 0:
            quant("p", T.pt[:], 0, 256, "pt0 pt1", "qp")
            V(ts(T.pp[:, 48:64], T.leg[:], -767.0, None, A.add), "leg", "pc")
            for k in range(R):
                V(cp(T.mf[:, 16 * k:16 * k + 16], T["mi%d" % k][:]), "mi%d" % k, "mf%d" % k)
        mm("k1", "p", 128, "ft", 0, 128, "qp qft")
        mm("k0", "p", 0, "ft", 0, 128, "qp qft")
        V(tt(L[0], F1, T.leg[:], A.mult), "ft2 leg", "l0")
        V(tt(L[1], F2, F3, A.add), "ft0 ft1", "l1")
        V(tt(L[2], L[1], T.mf[:, 16 * t:16 * t + 16], A.mult), "l1 mf%d" % t, "l2")
        V(scan(T.cum[:], T.k1[:, 0:64], T.zero[:, 0:64], 0.0, A.add, A.add), "k1 zero", "cum")
        V(tt(T.pp[:, 0:48], T.cum[:, 0:48], T.k0[:, 0:48], A.add), "cum k0", "pp")
        V(tt(T.m32[:], T.pp[:, 0:32], T.pp[:, 32:64], A.min), "pp pc", "m32")
        V(tt(T.m16[:], T.m32[:, 0:16], T.m32[:, 16:32], A.min), "m32", "m16")
        V(ts(T.pos[:], T.m16[:], 1023.0, None, A.add), "m16", "pos")
        V(cp(T.sl[:, 0:512].indirect(T.pos[:, 0:16]), T.row[:, 0:256]), "pos row", "sl")
        own(T.sl[:, 0:96], 96, "sl")
        wrap(T.wa[:, 0:96], 96, "wa")
        V(cp(T["slot%d" % t][:, 0:6], T.wb[:, 15:96:16]), "wb", "slot")
        order("G", [writer["slot"]])
        g.remote_dma(T["land%d" % t][:], T["slot%d" % t][:], T.sem["al%d" % t], T.sem.loc, pid, rid, mask)
        V(tt(L[3], T.cum[:, 48:64], T.k0[:, 48:64], A.add), "cum k0", "l3")
        V(tt(L[5], L[0], L[2], A.add), "l0 l2", "l5")
        V(ts(L[4], L[3], T.cum[:, 47:48], 1279.0, A.subtract, A.add), "l3 cum", "l4")
        V(ts(L[6], L[4], 352.0, -96.0, A.is_ge, A.mult), "l4", "l6")
        V(ts(L[7], L[4], 448.0, -96.0, A.is_ge, A.mult), "l4", "l7")
        V(tt(L[8], L[4], L[6], A.add), "l4 l6", "l8")
        V(tt(L[9], L[8], L[7], A.add), "l8 l7", "l9")
        V(tt(L[10], L[9], F4, A.mult), "l9 ft3", "l10")
        V(tt(L[11], L[5], L[10], A.add), "l5 l10", "l11")
        for b in range(4):
            V(ts(T["off%d" % b][:], L[11], 4.0, float(b), A.mult, A.add), "l11", "off%d" % b)
        if t == 0:
            V(cp(T.iv[:, 0:256].indirect(mo), T.row[:, 0:256]), "row" + mot, "iv")
            own(T.iv[:], 256, "iv")
            wrap(T.wa[:], 256, "wa")
            V(cp(T.inv0[:, 0:16], T.wb[:, 15:256:16]), "wb", "inv0")
            for k in (1, 2):
                n = 16 * k
                V(cp(T["mo%d" % k][:], T["mi%d" % k][:]), "mi%d" % k, "mo%d" % k)
                dma("S", T["inv%d" % k][0:128 - n, :], T.inv0[n:128, :], "ld_inv", "inv0", "inv%da" % k)
                dma("S", T["inv%d" % k][128 - n:128, :], T.inv0[0:n, :], "ld_inv", "inv0", "inv%d" % k)
            writer["inv1"] = writer["inv2"]
        elif t == 1:
            quant("v", T.v0[:], 0, 128, "v0", "qv")
        if t == R - 1:
            V(tt(T.d[:], T.lic2[:, 0:256].indirect(mo), T.tb[:, even], A.max), "lic2a lic2b tbv" + mot, "d")
        writer["hh"] = ("ah%d" % t, 2 * neng, {})
        writer["land"] = ("al%d" % t, neng, {})
        for b in range(4):
            mm("b%d" % b, "e", 128 * b, "h%d" % t, 0, 256, "qe hh")
            act(T["hp%d" % b][:, 0:256], T["b%d" % b][:, 0:256], "b%d" % b, "hp%d" % b)
        if t == R - 1:
            act(T.wrow[:], T.d[:], "d", "wrow", bias=11.0, scale=-8.0)
            dma("S", T.wv[:], T.wrow[0:128:16, :], "st", "wrow")
        for b in (0, 2, 1, 3):
            src, out = T["hp%d" % b][:, 0:272].indirect(T["land%d" % t][:, 0:6]), T.fg[:, 1024 + b:1408:4]
            r, w = "hp%d hz%d land" % (b, b), "g%d" % b
            if b < 2:
                V(cp(out, src), r, w)
            else:
                act(out, src, r, w)
        for b in (0, 2, 1, 3):
            src, out = T.fg[:, 0:1408].indirect(T["off%d" % b][:, 0:16]), T.z[:, b:1024:4]
            r, w = "f0 f1 f2 f3 g0 g1 g2 g3 off%d" % b, "z%d" % b
            if b < 2:
                V(cp(out, src), r, w)
            else:
                act(out, src, r, w)
        quant("z", T.z[:], 0, 256, "z0 z1 z2 z3", "qz")
        for b in range(4):
            mm("b%d" % b, "w", 128 * b, "z", 0, 256, "qw sw qz")
        for b in (0, 1):
            V(ts(T["z32%d" % b][:], T.z[:, b:1024:4], 32.0, None, A.mult), "z%d" % b, "z32%d" % b)
        for b in (2, 3):
            act(T["z32%d" % b][:], T.z[:, b:1024:4], "z%d" % b, "z32%d" % b, scale=32.0)
        for b in range(4):
            V(tt(T["tt%d" % b][:], T["b%d" % b][:, 0:256], T["z32%d" % b][:], A.add), "b%d z32%d" % (b, b), "tt%d" % b)
        for h in (0, 1):
            for b in range(4):
                src = T["tt%d" % b][:, 0:256].indirect(T["inv%d" % t][:, 8 * h:8 * h + 8])
                out, r, w = T.xt[:, 512 * h + b:512 * h + 512:4], "inv%d tt%d" % (t, b), "xs%d%d" % (b, h)
                if b == 3:
                    V(ts(out, src, 0.03125, None, A.mult), r, w)
                else:
                    act(out, src, r, w, scale=0.03125)
            quant_x(h, T.xt, " ".join(xs[4 * h:4 * h + 4]))
    for h in (0, 1):
        dma("S", T.oc[:, 512 * h:512 * h + 512], T.qx[:, 128 * h:128 * h + 128].bitcast(dt.uint8), "st", "qx%d" % h)
        mm("k%d" % h, "v", 0, "x", 128 * h, 128 * h + 128, "qv qx%d" % h)
    for k in range(4):
        dma("A", T.osc[4 * k:4 * k + 4, :], T.sx[32 * k:32 * k + 4, :], "st2", "qx0 qx1")
    for h in (0, 1):
        V(cp(T.yb[:, 128 * h:128 * h + 128], T["k%d" % h][:, 0:128]), "k%d" % h, "yb%d" % h)
        dma("S", T.y[:, 128 * h:128 * h + 128], T.yb[:, 128 * h:128 * h + 128], "st", "yb%d" % h)
    g.wait_ge(T.sem.loc, 3 * R * neng)
    for s in sorted(count):
        g.wait_ge(T.sem[s], count[s])
